import numpy as np
import ml_dtypes


def mxq(x, axis, fmt="e4m3"):
    dtype, down = {"e4m3": (ml_dtypes.float8_e4m3fn, 7), "e5m2": (ml_dtypes.float8_e5m2, 14)}[fmt]
    v = np.moveaxis(np.asarray(x, np.float32).astype(ml_dtypes.bfloat16).astype(np.float64), axis, -1)
    blocks = v.reshape(v.shape[:-1] + (-1, 32))
    amax = np.abs(blocks).max(-1, keepdims=True)
    byte = np.maximum(np.where(amax > 0, np.frexp(amax)[1] - 1 + 127, 0) - down, 1)
    scale = np.exp2(byte - 127.0)
    codes = (blocks / scale).astype(np.float32).astype(dtype).astype(np.float64)
    return np.moveaxis((codes * scale).reshape(v.shape), -1, axis)


WIDE = False


def mx_kscale(k):
    if not WIDE:
        return np.ones(k)
    levels = np.array([10, -10, 5, -5, 0])
    if k % 512:
        return np.exp2(np.random.permutation(np.resize(levels, k // 32))).repeat(32)
    a = np.empty((k // 512, 16))
    for p in range(k // 512):
        a[p, :8] = np.random.permutation(np.resize(levels, 8))
        for g in range(8):
            far = levels[np.abs(levels - a[p, g]) >= 10]
            a[p, g + 8] = far[np.random.randint(len(far))]
    return np.exp2(a.ravel()).repeat(32)


BF16 = ml_dtypes.bfloat16


def bf(x):
    return np.asarray(x, np.float32).astype(BF16)


def f64(x):
    return np.asarray(x).astype(np.float64)


E2M1 = np.array([0.0, 0.5, 1.0, 1.5, 2.0, 3.0, 4.0, 6.0, -0.0, -0.5, -1.0, -1.5, -2.0, -3.0, -4.0, -6.0])


def pack_weight(w, fmt):
    k, n = w.shape
    w = f64(bf(w)).reshape(k // 32, 32, n)
    amax = np.abs(w).max(1)
    if fmt == "e4m3":
        byte = np.frexp(amax)[1] - 1 + 127 - 7
    else:
        mant, ex = np.frexp(amax / 6.0)
        byte = np.where(mant > 0.5, ex, ex - 1) + 127
    byte = np.clip(np.where(amax > 0, byte, 1), 1, 254)
    scaled = (w * np.exp2(127.0 - byte)[:, None, :]).reshape(k, n).astype(np.float32)
    by_word = np.ascontiguousarray(scaled.reshape(k // 512, 128, 4, n).transpose(0, 1, 3, 2))
    if fmt == "e4m3":
        words = by_word.astype(ml_dtypes.float8_e4m3fn).view(np.uint8)
    else:
        c = by_word.astype(ml_dtypes.float4_e2m1fn).view(np.uint8) & 0xF
        words = c[..., 0::2] | (c[..., 1::2] << 4)
    return np.ascontiguousarray(words), np.ascontiguousarray(byte.astype(np.uint8).reshape(k // 512, 16, n))


def unpack_weight(words, scales, fmt):
    g, p, n, _ = words.shape
    if fmt == "e4m3":
        vals = np.ascontiguousarray(words).view(ml_dtypes.float8_e4m3fn).astype(np.float64)
    else:
        nib = np.empty((g, p, n, 4), np.uint8)
        nib[..., 0::2] = words & 0xF
        nib[..., 1::2] = words >> 4
        vals = E2M1[nib]
    vals = vals * np.repeat(np.exp2(scales.astype(np.float64) - 127.0), 8, axis=1)[..., None]
    return vals.transpose(0, 1, 3, 2).reshape(g * 512, n)

E4M3FN = np.array([(-1.0 if i & 128 else 1.0) * ((1.0 + (i & 7) / 8.0) * 2.0 ** (((i >> 3) & 15) - 7) if i & 120 else (i & 7) * 2.0 ** -9) for i in range(256)])


def e4m3fn_bytes(y):
    return np.clip(np.asarray(y, np.float64), -448.0, 448.0).astype(np.float32).astype(ml_dtypes.float8_e4m3fn).view(np.uint8)


def e4m3fn_values(b):
    return E4M3FN[b]


R, S, D, F, O = 256, 8, 512, 512, 1024


def softplus(v):
    return np.maximum(v, 0.0) + np.log1p(np.exp(-np.abs(v)))


def transmittance(tau):
    depth = np.cumsum(tau, axis=1)
    start = np.zeros_like(tau[:, :1, :])
    return np.exp(-np.concatenate([start, depth], axis=1))


def draw0():
    s, t = mx_kscale(D), mx_kscale(F)
    x = bf(np.random.standard_normal((R, S, D)) * s)
    we_words, we_scales = pack_weight(np.random.standard_normal((D, F)) / np.sqrt(D) / s[:, None], "e4m3")
    ws_words, ws_scales = pack_weight(np.random.standard_normal((D, F)) / np.sqrt(D) / s[:, None], "e4m3")
    dl = bf(np.random.uniform(0.8, 4.0, (R, S)) / S)
    bg = bf(np.random.standard_normal((R, F)))
    band = bf((1.0 + 0.1 * np.random.standard_normal(F)) * t)
    wm_words, wm_scales = pack_weight(np.random.standard_normal((F, O)) / np.sqrt(F) / t[:, None], "e4m3")
    return {
        "x": x,
        "we_words": we_words,
        "we_scales": we_scales,
        "ws_words": ws_words,
        "ws_scales": ws_scales,
        "dl": dl,
        "bg": bg,
        "band": band,
        "wm_words": wm_words,
        "wm_scales": wm_scales,
    }


def core(x, we_words, we_scales, ws_words, ws_scales, dl, bg, band, wm_words, wm_scales):
    xq = mxq(f64(x), 2, "e4m3")
    e = xq @ unpack_weight(we_words, we_scales, "e4m3")
    tau = f64(dl)[:, :, None] * softplus(xq @ unpack_weight(ws_words, ws_scales, "e4m3"))
    tr = transmittance(tau)
    c = np.sum(tr[:, :-1, :] * (1.0 - np.exp(-tau)) * e, axis=1) + tr[:, -1, :] * f64(bg)
    return mxq(c * f64(band)[None, :], 1, "e4m3") @ unpack_weight(wm_words, wm_scales, "e4m3")


def setup_inputs():
    drawn = draw0()
    full = np.asarray(drawn['x']).astype(np.float64)
    scale = (np.abs(full).reshape(256, 8, 4, 128).max(axis=(3,)) / 448.0).astype(np.float32)
    given = {}
    for key, value in drawn.items():
        if key == 'x':
            given['x_bytes'] = e4m3fn_bytes(full / np.repeat(scale.astype(np.float64), 128, axis=2))
            given['x_scale'] = scale
        else:
            given[key] = value
    return given


def reference(x_bytes, x_scale, we_words, we_scales, ws_words, ws_scales, dl, bg, band, wm_words, wm_scales):
    return core(e4m3fn_values(x_bytes) * np.repeat(x_scale.astype(np.float64), 128, axis=2), we_words, we_scales, ws_words, ws_scales, dl, bg, band, wm_words, wm_scales)

@@ -1,0 +1,307 @@
+from contextlib import ExitStack
+
+import concourse.mybir as mybir
+from concourse.masks import make_identity
+
+F32 = mybir.dt.float32
+BF16 = mybir.dt.bfloat16
+I32 = mybir.dt.int32
+U32 = mybir.dt.uint32
+U8 = mybir.dt.uint8
+F8 = mybir.dt.float8_e4m3fn
+X4 = mybir.dt.float8_e4m3fn_x4
+ALU = mybir.AluOpType
+ACT = mybir.ActivationFunctionType
+
+R, S, D, F, O = 256, 8, 512, 512, 1024
+P = 128
+RT = R // P
+FLOPS = 2 * R * S * D * F * 2 + 2 * R * F * O
+
+N_A = 4
+DQ_S = (3, 2, 1, 0, 0, 0, 2, 0)
+LEAD = 3
+DR_S = (0,)
+M_G = ()
+EV = (0, 2, 6, 0, 0, 0, 0, 0)
+SPB = (0, 0, 1, 1, 1, 1, 0, 0)
+CLAMP = 40.0
+
+
+def tile_spectralextinctionemissioncompositing_d1p_kernel(
+    tc, x_bytes, x_scale, we_words, we_scales, ws_words, ws_scales, dl, bg, band, wm_words, wm_scales, out
+):
+    nc = tc.nc
+    with ExitStack() as ctx:
+        keep = ctx.enter_context(tc.tile_pool(name="keep", bufs=1))
+        work = ctx.enter_context(tc.tile_pool(name="work", bufs=2))
+        psum = ctx.enter_context(tc.psum_pool(name="psum", bufs=2))
+        ctx.enter_context(tc.manual_schedule())
+
+        warm = keep.tile([P, 1], F32, name="warm")
+        nc.vector.memset(warm[:], 0.0)
+        nc.scalar.activation(out=warm[:], in_=warm[:], func=ACT.Exp)
+
+        xs = keep.tile([P, RT, S * 4], F32, name="xs")
+        nc.sync.dma_start(out=xs[:], in_=x_scale.rearrange("(c p) s j -> p c (s j)", p=P))
+        xv = x_bytes.rearrange("(c p) s k -> p c s k", p=P)
+        x8 = []
+
+        def load_x(s0):
+            t = keep.tile([P, RT, 2, D], U8, name="x8_%d" % s0)
+            nc.sync.dma_start(out=t[:], in_=xv[:, :, s0 : s0 + 2, :])
+            return t
+
+        x_tiles = {}
+        x_tiles[6] = load_x(6)
+
+        def scale_tile(nm, width):
+            t = keep.tile([P, width], U8, name=nm, align_bytes=64)
+            nc.vector.memset(t[:].bitcast(I32), 0)
+            return t
+
+        def load_words(nm, src, width):
+            t = keep.tile([P, width], U32, name=nm, align_bytes=64)
+            nc.sync.dma_start(out=t[:].bitcast(I32), in_=src[0].rearrange("p n t -> p (n t)").bitcast(I32))
+            return t
+
+        def load_scales(t, src):
+            for q in range(4):
+                nc.sync.dma_start(
+                    out=t[32 * q : 32 * q + 4, :].bitcast(I32), in_=src[0, 4 * q : 4 * q + 4, :].bitcast(I32)
+                )
+
+        ws_s = scale_tile("ws_s", F)
+        ws_w = load_words("ws_w", ws_words, F)
+        load_scales(ws_s, ws_scales)
+        x_tiles[4] = load_x(4)
+        dl_b = keep.tile([P, RT, S], BF16, name="dl_b")
+        nc.sync.dma_start(out=dl_b[:], in_=dl.rearrange("(c p) s -> p c s", p=P))
+        x_tiles[2] = load_x(2)
+        x_tiles[0] = load_x(0)
+        we_s = scale_tile("we_s", F)
+        we_w = load_words("we_w", we_words, F)
+        load_scales(we_s, we_scales)
+        bg_b = keep.tile([P, RT, F], BF16, name="bg_b")
+        nc.sync.dma_start(out=bg_b[:], in_=bg.rearrange("(c p) f -> p c f", p=P))
+        band_b = keep.tile([P, F], BF16, name="band_b")
+        nc.sync.dma_start(out=band_b[:], in_=band.partition_broadcast(P))
+        wm_s = scale_tile("wm_s", O)
+        wm_w = load_words("wm_w", wm_words, O)
+        load_scales(wm_s, wm_scales)
+
+        ident = keep.tile([P, P], F32, name="ident")
+        make_identity(nc, ident[:])
+
+        ndl = keep.tile([P, RT * S], F32, name="ndl")
+
+        w_t = [keep.tile([P, RT, F], F32, name="w%d" % s) for s in range(S)]
+        cx = [keep.tile([P, RT * P], U32, name="cx%d" % s, align_bytes=64) for s in range(S)]
+        sx = [keep.tile([P, RT * P], U8, name="sx%d" % s, align_bytes=64) for s in range(S)]
+        xb = {}
+        gr = {}
+
+        def deq(s, blocks, engine):
+            if s not in xb:
+                xb[s] = work.tile([P, RT, D], BF16, name="xb", tag="xb", bufs=4)
+            src = x_tiles[s // 2 * 2]
+            for b in blocks:
+                c, j = divmod(b, 4)
+                o = xb[s][:, c, 128 * j : 128 * (j + 1)]
+                i = src[:, c, s % 2, 128 * j : 128 * (j + 1)].bitcast(F8)
+                sc = xs[:, c, 4 * s + j : 4 * s + j + 1]
+                if engine is nc.scalar:
+                    nc.scalar.activation(out=o, in_=i, func=ACT.Copy, scale=sc)
+                else:
+                    nc.vector.tensor_scalar(out=o, in0=i, scalar1=sc, scalar2=None, op0=ALU.mult)
+
+        def turn_words(src, dst):
+            words = src.bitcast(F32)
+            for u in range(2):
+                nc.tensor.transpose(dst[:, u, :], words[:, u : D // 2 : 2], ident[:])
+
+        xt = {}
+
+        def turn(s):
+            xt[s] = psum.tile([P, RT, 2, P], F32, name="xt", tag="xt", bufs=2)
+            for c in range(RT):
+                turn_words(xb[s][:, c, :], xt[s][:, c])
+
+        def drain(s, engine):
+            gr[s] = work.tile([P, RT * P * 2], F32, name="gr", tag="gr", bufs=2, align_bytes=64)
+            copy = nc.scalar.copy if engine is nc.scalar else nc.vector.tensor_copy
+            copy(
+                out=gr[s][:].rearrange("p (c r u) -> p c r u", c=RT, u=2),
+                in_=xt[s][:].rearrange("p c u r -> p c r u"),
+            )
+
+        def quant(s):
+            nc.vector.quantize_mx(out=cx[s][:].bitcast(X4), scales=sx[s][:], in_=gr[s][:].bitcast(BF16))
+
+        def mm(tag, bufs, s, c, w, sc):
+            t = psum.tile([P, F], F32, name=tag, tag=tag, bufs=bufs)
+            cols = slice(c * P, (c + 1) * P)
+            nc.tensor.matmul_mx(
+                out=t[:],
+                lhsT=cx[s][:, cols].bitcast(X4),
+                lhsT_scale=sx[s][:, cols],
+                rhs=w[:].bitcast(X4),
+                rhs_scale=sc[:],
+                start=True,
+                stop=True,
+            )
+            return t
+
+        def exp_v(s, c):
+            v = mm("v", 3, s, c, ws_w, ws_s)
+            nc.scalar.activation(out=w_t[s][:, c, :], in_=v[:], func=ACT.Exp)
+
+        def log1p(s):
+            t = w_t[s][:].rearrange("p c f -> p (c f)")
+            nc.scalar.activation(out=t, in_=t, func=ACT.Ln, bias=1.0)
+
+        def softplus(s, c):
+            v = mm("v", 3, s, c, ws_w, ws_s)
+            t = w_t[s][:, c, :]
+            nc.vector.scalar_tensor_tensor(out=t, in0=t, scalar=CLAMP, in1=v[:], op0=ALU.min, op1=ALU.max)
+
+        def exp_tau(s, c):
+            t = w_t[s][:, c, :]
+            nc.scalar.activation(out=t, in_=t, func=ACT.Exp, scale=ndl[:, c * S + s : c * S + s + 1])
+
+        q_t = {}
+        h_t = [bg_b[:]]
+
+        def step_q(s):
+            q_t[s] = work.tile([P, RT, F], F32, name="q", tag="q", bufs=3)
+            for c in range(RT):
+                e = mm("e", 3, s, c, we_w, we_s)
+                nc.vector.scalar_tensor_tensor(
+                    out=q_t[s][:, c, :], in0=w_t[s][:, c, :], scalar=1.0, in1=e[:], op0=ALU.subtract, op1=ALU.mult
+                )
+
+        def step_m(s, c):
+            t = w_t[s][:, c, :]
+            nc.vector.tensor_tensor(out=t, in0=t, in1=h_t[0][:, c, :], op=ALU.mult)
+
+        def step_h(s, c, h):
+            nc.vector.tensor_tensor(out=h[:, c, :], in0=w_t[s][:, c, :], in1=q_t[s][:, c, :], op=ALU.subtract)
+
+        def new_h():
+            return work.tile([P, RT, F], F32, name="h", tag="h", bufs=2)
+
+        fin = {}
+
+        def finish_turn(c):
+            cb = work.tile([P, F], BF16, name="cb%d" % c, tag="cb%d" % c, bufs=1)
+            nc.vector.tensor_tensor(out=cb[:], in0=h_t[0][:, c, :], in1=band_b[:], op=ALU.mult)
+            ct = psum.tile([P, 2, P], F32, name="ct", tag="xt", bufs=2)
+            turn_words(cb[:], ct)
+            fin[c] = ct
+
+        def finish_quant(c):
+            g = work.tile([P, P * 2], F32, name="cg", tag="cg", bufs=2, align_bytes=64)
+            nc.scalar.copy(out=g[:].rearrange("p (r u) -> p r u", u=2), in_=fin[c][:].rearrange("p u r -> p r u"))
+            cc = work.tile([P, P], U32, name="cc", tag="cc", bufs=2, align_bytes=64)
+            cs = work.tile([P, P], U8, name="cs", tag="cs", bufs=2, align_bytes=64)
+            nc.vector.quantize_mx(out=cc[:].bitcast(X4), scales=cs[:], in_=g[:].bitcast(BF16))
+            fin[c] = (cc, cs)
+
+        def finish_out(c):
+            cc, cs = fin[c]
+            for n in range(2):
+                cols = slice(n * 512, (n + 1) * 512)
+                o = psum.tile([P, 512], F32, name="o", tag="e", bufs=3)
+                nc.tensor.matmul_mx(
+                    out=o[:],
+                    lhsT=cc[:].bitcast(X4),
+                    lhsT_scale=cs[:],
+                    rhs=wm_w[:, cols].bitcast(X4),
+                    rhs_scale=wm_s[:, cols],
+                    start=True,
+                    stop=True,
+                )
+                ob = work.tile([P, 512], F32, name="ob%d" % n, tag="ob%d" % n, bufs=2)
+                if n == 0:
+                    nc.scalar.copy(out=ob[:], in_=o[:])
+                else:
+                    nc.vector.tensor_copy(out=ob[:], in_=o[:])
+                nc.sync.dma_start(out=out[c * P : (c + 1) * P, cols], in_=ob[:])
+
+        order = list(range(S - 1, -1, -1))
+        first, second = order[:N_A], order[N_A:]
+
+        def deq_s(i):
+            if i < S:
+                deq(order[i], range(8 - DQ_S[i], 8), nc.scalar)
+
+        def deq_v(i, part):
+            if i < S:
+                n = 8 - DQ_S[i]
+                deq(order[i], range(0, n // 2) if part == 0 else range(n // 2, n), nc.vector)
+
+        for i in range(LEAD):
+            deq_s(i)
+        deq_v(0, 0)
+        deq_v(0, 1)
+        turn(order[0])
+        for i in range(S):
+            deq_s(i + LEAD)
+            deq_v(i + 1, 0)
+            drain(order[i], nc.scalar if i in DR_S else nc.vector)
+            deq_v(i + 1, 1)
+            quant(order[i])
+            if i + 1 < S:
+                turn(order[i + 1])
+            if i < N_A:
+                for c in range(RT):
+                    exp_v(order[i], c)
+            if i == N_A - 1:
+                nc.vector.tensor_scalar(
+                    out=ndl[:], in0=dl_b[:].rearrange("p c s -> p (c s)"), scalar1=-1.0, scalar2=None, op0=ALU.mult
+                )
+                for s in first:
+                    log1p(s)
+        for s in first:
+            for c in range(RT):
+                softplus(s, c)
+        for s in first:
+            for c in range(RT):
+                exp_tau(s, c)
+        ev = [(s, c) for s in second for c in range(RT)]
+        todo = list(second)
+        both = slice(0, RT)
+        step_q(order[0])
+        for i in range(S):
+            s = order[i]
+            for x, c in ev[: EV[i]]:
+                exp_v(x, c)
+            if ev and EV[i] >= len(ev):
+                for x in second:
+                    log1p(x)
+            ev = ev[EV[i] :]
+            h = new_h()
+            if i + 1 < S:
+                step_m(s, both)
+                nq = order[i + 1]
+                if i + 1 != N_A:
+                    step_q(nq)
+                step_h(s, both, h)
+            else:
+                for c in range(RT):
+                    step_m(s, c)
+                for c in range(RT):
+                    step_h(s, c, h)
+            h_t[0] = h[:]
+            for x in todo[: SPB[i]]:
+                for c in range(RT):
+                    softplus(x, c)
+            for x in todo[: SPB[i]]:
+                for c in range(RT):
+                    exp_tau(x, c)
+            todo = todo[SPB[i] :]
+            if i + 1 == N_A:
+                step_q(order[i + 1])
+        for step in (finish_turn, finish_quant, finish_out):
+            for c in range(RT):
+                step(c)

@@ -18,13 +18,13 @@ P = 128
 RT = R // P
 FLOPS = 2 * R * S * D * F * 2 + 2 * R * F * O
 
-N_A = 4
-DQ_S = (3, 2, 1, 0, 0, 0, 2, 0)
+BATCHES = (8,)
+DQ_S = (2, 4, 6, 7, 0, 2, 1, 2)
 LEAD = 3
-DR_S = (0,)
-M_G = ()
-EV = (0, 2, 6, 0, 0, 0, 0, 0)
-SPB = (0, 0, 1, 1, 1, 1, 0, 0)
+DR_S = ()
+D_G = (1, 2, 3, 4, 5, 8)
+V_ORDER = 'xxxxxxxxddcdcdcdcddccdDcpppcppDpDpp'
+PACE = 3
 CLAMP = 40.0
 
 
@@ -53,7 +53,7 @@ def tile_spectralextinctionemissioncompositing_d1p_kernel(
             return t
 
         x_tiles = {}
-        x_tiles[6] = load_x(6)
+        x_tiles[0] = load_x(0)
 
         def scale_tile(nm, width):
             t = keep.tile([P, width], U8, name=nm, align_bytes=64)
@@ -74,26 +74,24 @@ def tile_spectralextinctionemissioncompositing_d1p_kernel(
         ws_s = scale_tile("ws_s", F)
         ws_w = load_words("ws_w", ws_words, F)
         load_scales(ws_s, ws_scales)
-        x_tiles[4] = load_x(4)
+        x_tiles[2] = load_x(2)
         dl_b = keep.tile([P, RT, S], BF16, name="dl_b")
         nc.sync.dma_start(out=dl_b[:], in_=dl.rearrange("(c p) s -> p c s", p=P))
-        x_tiles[2] = load_x(2)
-        x_tiles[0] = load_x(0)
+        x_tiles[4] = load_x(4)
+        x_tiles[6] = load_x(6)
         we_s = scale_tile("we_s", F)
         we_w = load_words("we_w", we_words, F)
         load_scales(we_s, we_scales)
         bg_b = keep.tile([P, RT, F], BF16, name="bg_b")
         nc.sync.dma_start(out=bg_b[:], in_=bg.rearrange("(c p) f -> p c f", p=P))
-        band_b = keep.tile([P, F], BF16, name="band_b")
-        nc.sync.dma_start(out=band_b[:], in_=band.partition_broadcast(P))
+        band_b = keep.tile([P, 4], BF16, name="band_b")
+        nc.sync.dma_start(out=band_b[:], in_=band.rearrange("(p t) -> p t", t=4))
         wm_s = scale_tile("wm_s", O)
         wm_w = load_words("wm_w", wm_words, O)
         load_scales(wm_s, wm_scales)
 
         ident = keep.tile([P, P], F32, name="ident")
         make_identity(nc, ident[:])
-
-        ndl = keep.tile([P, RT * S], F32, name="ndl")
 
         w_t = [keep.tile([P, RT, F], F32, name="w%d" % s) for s in range(S)]
         cx = [keep.tile([P, RT * P], U32, name="cx%d" % s, align_bytes=64) for s in range(S)]
@@ -103,7 +101,7 @@ def tile_spectralextinctionemissioncompositing_d1p_kernel(
 
         def deq(s, blocks, engine):
             if s not in xb:
-                xb[s] = work.tile([P, RT, D], BF16, name="xb", tag="xb", bufs=4)
+                xb[s] = work.tile([P, RT, D], BF16, name="xb", tag="xb", bufs=5)
             src = x_tiles[s // 2 * 2]
             for b in blocks:
                 c, j = divmod(b, 4)
@@ -123,7 +121,7 @@ def tile_spectralextinctionemissioncompositing_d1p_kernel(
         xt = {}
 
         def turn(s):
-            xt[s] = psum.tile([P, RT, 2, P], F32, name="xt", tag="xt", bufs=2)
+            xt[s] = psum.tile([P, RT, 2, P], F32, name="xt", tag="xe", bufs=4)
             for c in range(RT):
                 turn_words(xb[s][:, c, :], xt[s][:, c])
 
@@ -153,7 +151,7 @@ def tile_spectralextinctionemissioncompositing_d1p_kernel(
             return t
 
         def exp_v(s, c):
-            v = mm("v", 3, s, c, ws_w, ws_s)
+            v = mm("v", 2, s, c, ws_w, ws_s)
             nc.scalar.activation(out=w_t[s][:, c, :], in_=v[:], func=ACT.Exp)
 
         def log1p(s):
@@ -161,57 +159,80 @@ def tile_spectralextinctionemissioncompositing_d1p_kernel(
             nc.scalar.activation(out=t, in_=t, func=ACT.Ln, bias=1.0)
 
         def softplus(s, c):
-            v = mm("v", 3, s, c, ws_w, ws_s)
+            v = mm("v", 2, s, c, ws_w, ws_s)
             t = w_t[s][:, c, :]
             nc.vector.scalar_tensor_tensor(out=t, in0=t, scalar=CLAMP, in1=v[:], op0=ALU.min, op1=ALU.max)
 
-        def exp_tau(s, c):
+        def depth(s, c):
             t = w_t[s][:, c, :]
-            nc.scalar.activation(out=t, in_=t, func=ACT.Exp, scale=ndl[:, c * S + s : c * S + s + 1])
-
-        q_t = {}
-        h_t = [bg_b[:]]
-
-        def step_q(s):
-            q_t[s] = work.tile([P, RT, F], F32, name="q", tag="q", bufs=3)
-            for c in range(RT):
-                e = mm("e", 3, s, c, we_w, we_s)
+            length = dl_b[:, c, s : s + 1]
+            if s == 0:
+                nc.vector.tensor_scalar(out=t, in0=t, scalar1=length, scalar2=None, op0=ALU.mult)
+            else:
                 nc.vector.scalar_tensor_tensor(
-                    out=q_t[s][:, c, :], in0=w_t[s][:, c, :], scalar=1.0, in1=e[:], op0=ALU.subtract, op1=ALU.mult
+                    out=t, in0=t, scalar=length, in1=w_t[s - 1][:, c, :], op0=ALU.mult, op1=ALU.add
                 )
 
-        def step_m(s, c):
-            t = w_t[s][:, c, :]
-            nc.vector.tensor_tensor(out=t, in0=t, in1=h_t[0][:, c, :], op=ALU.mult)
+        tr = [None] + [keep.tile([P, RT, F], F32, name="tr%d" % s) for s in range(1, S + 1)]
+        dr = [keep.tile([P, RT, F], F32, name="dr%d" % s) for s in range(S + 1)]
 
-        def step_h(s, c, h):
-            nc.vector.tensor_tensor(out=h[:, c, :], in0=w_t[s][:, c, :], in1=q_t[s][:, c, :], op=ALU.subtract)
+        def exp_depth(s):
+            nc.scalar.activation(out=tr[s + 1][:], in_=w_t[s][:], func=ACT.Exp, scale=-1.0)
 
-        def new_h():
-            return work.tile([P, RT, F], F32, name="h", tag="h", bufs=2)
+        def drop(s):
+            engine = nc.gpsimd if s in D_G else nc.vector
+            if s == 0:
+                engine.tensor_scalar(out=dr[0][:], in0=tr[1][:], scalar1=-1.0, scalar2=1.0, op0=ALU.mult, op1=ALU.add)
+            elif s < S:
+                engine.tensor_tensor(out=dr[s][:], in0=tr[s][:], in1=tr[s + 1][:], op=ALU.subtract)
+            else:
+                engine.tensor_tensor(out=dr[s][:], in0=tr[s][:], in1=bg_b[:], op=ALU.mult)
+
+        c_t = [psum.tile([P, 4, P], F32, name="c%d" % c, tag="c%d" % c, bufs=1) for c in range(RT)]
+        p_t = {}
+
+        def emit_e(s):
+            return [mm("xe", 4, s, c, we_w, we_s) for c in range(RT)]
+
+        def product(s, c, e):
+            p_t[c] = work.tile([P, F], F32, name="p%d" % c, tag="p%d" % c, bufs=3)
+            nc.vector.tensor_tensor(out=p_t[c][:], in0=dr[s][:, c, :], in1=e[c][:], op=ALU.mult)
+
+        def turn_add(s, c):
+            src = dr[s][:, c, :] if s == S else p_t[c][:]
+            for t in range(4):
+                nc.tensor.matmul(
+                    out=c_t[c][:, t, :],
+                    lhsT=src[:, t:F:4],
+                    rhs=ident[:],
+                    is_transpose=True,
+                    start=(s == 0 and t == 0),
+                    stop=(s == S and t == 3),
+                )
 
         fin = {}
 
-        def finish_turn(c):
-            cb = work.tile([P, F], BF16, name="cb%d" % c, tag="cb%d" % c, bufs=1)
-            nc.vector.tensor_tensor(out=cb[:], in0=h_t[0][:, c, :], in1=band_b[:], op=ALU.mult)
-            ct = psum.tile([P, 2, P], F32, name="ct", tag="xt", bufs=2)
-            turn_words(cb[:], ct)
-            fin[c] = ct
-
         def finish_quant(c):
-            g = work.tile([P, P * 2], F32, name="cg", tag="cg", bufs=2, align_bytes=64)
-            nc.scalar.copy(out=g[:].rearrange("p (r u) -> p r u", u=2), in_=fin[c][:].rearrange("p u r -> p r u"))
+            g = work.tile([P, F], BF16, name="cg", tag="cg", bufs=2, align_bytes=64)
+            nc.vector.tensor_tensor(
+                out=g[:].rearrange("p (r t) -> p r t", t=4),
+                in0=c_t[c][:].rearrange("p t r -> p r t"),
+                in1=band_b[:].unsqueeze(1).broadcast_to([P, P, 4]),
+                op=ALU.mult,
+            )
+            fin[c] = g
+
+        def finish_mx(c):
             cc = work.tile([P, P], U32, name="cc", tag="cc", bufs=2, align_bytes=64)
             cs = work.tile([P, P], U8, name="cs", tag="cs", bufs=2, align_bytes=64)
-            nc.vector.quantize_mx(out=cc[:].bitcast(X4), scales=cs[:], in_=g[:].bitcast(BF16))
+            nc.vector.quantize_mx(out=cc[:].bitcast(X4), scales=cs[:], in_=fin[c][:])
             fin[c] = (cc, cs)
 
         def finish_out(c):
             cc, cs = fin[c]
             for n in range(2):
                 cols = slice(n * 512, (n + 1) * 512)
-                o = psum.tile([P, 512], F32, name="o", tag="e", bufs=3)
+                o = psum.tile([P, 512], F32, name="o", tag="xe", bufs=4)
                 nc.tensor.matmul_mx(
                     out=o[:],
                     lhsT=cc[:].bitcast(X4),
@@ -228,80 +249,98 @@ def tile_spectralextinctionemissioncompositing_d1p_kernel(
                     nc.vector.tensor_copy(out=ob[:], in_=o[:])
                 nc.sync.dma_start(out=out[c * P : (c + 1) * P, cols], in_=ob[:])
 
-        order = list(range(S - 1, -1, -1))
-        first, second = order[:N_A], order[N_A:]
+        def deq_s(s):
+            if s < S:
+                deq(s, range(8 - DQ_S[s], 8), nc.scalar)
 
-        def deq_s(i):
-            if i < S:
-                deq(order[i], range(8 - DQ_S[i], 8), nc.scalar)
+        def deq_v(s, part):
+            if s < S:
+                n = 8 - DQ_S[s]
+                deq(s, range(0, n // 2) if part == 0 else range(n // 2, n), nc.vector)
 
-        def deq_v(i, part):
-            if i < S:
-                n = 8 - DQ_S[i]
-                deq(order[i], range(0, n // 2) if part == 0 else range(n // 2, n), nc.vector)
+        def prep(s):
+            deq_s(s + LEAD)
+            deq_v(s + 2, 0)
+            drain(s, nc.scalar if s in DR_S else nc.vector)
+            deq_v(s + 2, 1)
+            quant(s)
+            if s + 2 < S:
+                turn(s + 2)
 
-        for i in range(LEAD):
-            deq_s(i)
-        deq_v(0, 0)
-        deq_v(0, 1)
-        turn(order[0])
-        for i in range(S):
-            deq_s(i + LEAD)
-            deq_v(i + 1, 0)
-            drain(order[i], nc.scalar if i in DR_S else nc.vector)
-            deq_v(i + 1, 1)
-            quant(order[i])
-            if i + 1 < S:
-                turn(order[i + 1])
-            if i < N_A:
-                for c in range(RT):
-                    exp_v(order[i], c)
-            if i == N_A - 1:
-                nc.vector.tensor_scalar(
-                    out=ndl[:], in0=dl_b[:].rearrange("p c s -> p (c s)"), scalar1=-1.0, scalar2=None, op0=ALU.mult
-                )
-                for s in first:
-                    log1p(s)
-        for s in first:
+        def exp_both(s):
             for c in range(RT):
-                softplus(s, c)
-        for s in first:
-            for c in range(RT):
-                exp_tau(s, c)
-        ev = [(s, c) for s in second for c in range(RT)]
-        todo = list(second)
-        both = slice(0, RT)
-        step_q(order[0])
-        for i in range(S):
-            s = order[i]
-            for x, c in ev[: EV[i]]:
-                exp_v(x, c)
-            if ev and EV[i] >= len(ev):
-                for x in second:
-                    log1p(x)
-            ev = ev[EV[i] :]
-            h = new_h()
-            if i + 1 < S:
-                step_m(s, both)
-                nq = order[i + 1]
-                if i + 1 != N_A:
-                    step_q(nq)
-                step_h(s, both, h)
-            else:
+                exp_v(s, c)
+
+        s_order = []
+        s0 = 0
+        for n in BATCHES:
+            batch = range(s0, s0 + n)
+            s0 += n
+            s_order += [("E", s) for s in batch] + [("L", s) for s in batch] + [("X", s) for s in batch]
+        s_call = {"E": exp_both, "L": log1p, "X": exp_depth}
+        done = {"E": 0, "L": 0, "X": 0}
+        count = {"x": 0, "d": 0, "c": 0, "p": 0}
+
+        def advance_scalar(limit):
+            for k in range(limit):
+                if not s_order:
+                    return
+                kind, s = s_order[0]
+                if kind == "E" and s >= count["x"]:
+                    return
+                if kind == "X" and s >= count["c"]:
+                    return
+                s_order.remove(s_order[0])
+                s_call[kind](s)
+                done[kind] = s + 1
+                if kind == "X" and s in D_G:
+                    drop(s)
+                if kind == "X" and s == S - 1 and S in D_G:
+                    drop(S)
+
+        e_t = {}
+        for s in range(LEAD):
+            deq_s(s)
+        for s in range(2):
+            deq_v(s, 0)
+            deq_v(s, 1)
+            turn(s)
+        v_drops = [s for s in range(S + 1) if s not in D_G]
+        for op in V_ORDER:
+            if op == "D":
+                s = v_drops[0]
+                v_drops.remove(s)
+                while done["X"] <= min(s, S - 1):
+                    advance_scalar(1)
+                drop(s)
+                continue
+            s = count[op]
+            if op == "x":
+                prep(s)
+            if op == "d":
+                while done["L"] <= s:
+                    advance_scalar(1)
                 for c in range(RT):
-                    step_m(s, c)
+                    softplus(s, c)
+            if op == "c":
                 for c in range(RT):
-                    step_h(s, c, h)
-            h_t[0] = h[:]
-            for x in todo[: SPB[i]]:
+                    depth(s, c)
+            if op == "p":
+                while done["X"] <= s:
+                    advance_scalar(1)
+                if s == 0:
+                    e_t[0] = emit_e(0)
+                    e_t[1] = emit_e(1)
                 for c in range(RT):
-                    softplus(x, c)
-            for x in todo[: SPB[i]]:
+                    product(s, c, e_t[s])
+                if s + 2 < S:
+                    e_t[s + 2] = emit_e(s + 2)
                 for c in range(RT):
-                    exp_tau(x, c)
-            todo = todo[SPB[i] :]
-            if i + 1 == N_A:
-                step_q(order[i + 1])
-        for step in (finish_turn, finish_quant, finish_out):
+                    turn_add(s, c)
+            count[op] = s + 1
+            advance_scalar(PACE)
+        for c in range(RT):
+            turn_add(S, c)
+        for step in (finish_quant, finish_mx, finish_out):
             for c in range(RT):
                 step(c)

@@ -22,9 +22,9 @@ BATCHES = (8,)
 DQ_S = (2, 4, 6, 7, 0, 2, 1, 2)
 LEAD = 3
 DR_S = ()
-D_G = (1, 2, 3, 4, 5, 8)
-V_ORDER = 'xxxxxxxxddcdcdcdcddccdDcpppcppDpDpp'
-PACE = 3
+T_V = (1,)
+V_ORDER = "xxxxxxxxwddddddddgpTppppppp"
+PACE = 2
 CLAMP = 40.0
 
 
@@ -71,17 +71,17 @@ def tile_spectralextinctionemissioncompositing_d1p_kernel(
                     out=t[32 * q : 32 * q + 4, :].bitcast(I32), in_=src[0, 4 * q : 4 * q + 4, :].bitcast(I32)
                 )
 
-        ws_s = scale_tile("ws_s", F)
-        ws_w = load_words("ws_w", ws_words, F)
-        load_scales(ws_s, ws_scales)
+        ws_raw_s = scale_tile("ws_raw_s", F)
+        ws_raw_w = load_words("ws_raw_w", ws_words, F)
+        load_scales(ws_raw_s, ws_scales)
         x_tiles[2] = load_x(2)
         dl_b = keep.tile([P, RT, S], BF16, name="dl_b")
         nc.sync.dma_start(out=dl_b[:], in_=dl.rearrange("(c p) s -> p c s", p=P))
         x_tiles[4] = load_x(4)
         x_tiles[6] = load_x(6)
-        we_s = scale_tile("we_s", F)
-        we_w = load_words("we_w", we_words, F)
-        load_scales(we_s, we_scales)
+        we_raw_s = scale_tile("we_raw_s", F)
+        we_raw_w = load_words("we_raw_w", we_words, F)
+        load_scales(we_raw_s, we_scales)
         bg_b = keep.tile([P, RT, F], BF16, name="bg_b")
         nc.sync.dma_start(out=bg_b[:], in_=bg.rearrange("(c p) f -> p c f", p=P))
         band_b = keep.tile([P, 4], BF16, name="band_b")
@@ -89,6 +89,23 @@ def tile_spectralextinctionemissioncompositing_d1p_kernel(
         wm_s = scale_tile("wm_s", O)
         wm_w = load_words("wm_w", wm_words, O)
         load_scales(wm_s, wm_scales)
+
+        ws_w = keep.tile([P, F], U32, name="ws_w", align_bytes=64)
+        ws_s = keep.tile([P, F], U8, name="ws_s", align_bytes=64)
+        we_w = keep.tile([P, F], U32, name="we_w", align_bytes=64)
+        we_s = keep.tile([P, F], U8, name="we_s", align_bytes=64)
+
+        def permute(dst, src):
+            nc.vector.tensor_copy(
+                out=dst.rearrange("p (t q) -> p t q", t=4), in_=src.rearrange("p (q t) -> p t q", t=4)
+            )
+
+        def permute_weight(w, s, raw_w, raw_s):
+            permute(w[:].bitcast(I32), raw_w[:].bitcast(I32))
+            permute(s[:], raw_s[:])
+
+        nband = keep.tile([P, 4], F32, name="nband")
+        ndl = keep.tile([P, RT * S], F32, name="ndl")
 
         ident = keep.tile([P, P], F32, name="ident")
         make_identity(nc, ident[:])
@@ -159,34 +176,21 @@ def tile_spectralextinctionemissioncompositing_d1p_kernel(
             nc.scalar.activation(out=t, in_=t, func=ACT.Ln, bias=1.0)
 
         def softplus(s, c):
-            v = mm("v", 2, s, c, ws_w, ws_s)
+            v = mm("xe", 4, s, c, ws_w, ws_s)
             t = w_t[s][:, c, :]
             nc.vector.scalar_tensor_tensor(out=t, in0=t, scalar=CLAMP, in1=v[:], op0=ALU.min, op1=ALU.max)
 
-        def depth(s, c):
-            t = w_t[s][:, c, :]
-            length = dl_b[:, c, s : s + 1]
-            if s == 0:
-                nc.vector.tensor_scalar(out=t, in0=t, scalar1=length, scalar2=None, op0=ALU.mult)
-            else:
-                nc.vector.scalar_tensor_tensor(
-                    out=t, in0=t, scalar=length, in1=w_t[s - 1][:, c, :], op0=ALU.mult, op1=ALU.add
-                )
+        tr = [None, w_t[0]] + [keep.tile([P, RT, F], F32, name="tr%d" % s) for s in range(2, S + 1)]
+        d7 = keep.tile([P, RT, F], F32, name="d7")
 
-        tr = [None] + [keep.tile([P, RT, F], F32, name="tr%d" % s) for s in range(1, S + 1)]
-        dr = [keep.tile([P, RT, F], F32, name="dr%d" % s) for s in range(S + 1)]
+        def exp_tau(s):
+            for c in range(RT):
+                t = w_t[s][:, c, :]
+                nc.scalar.activation(out=t, in_=t, func=ACT.Exp, scale=ndl[:, c * S + s : c * S + s + 1])
 
-        def exp_depth(s):
-            nc.scalar.activation(out=tr[s + 1][:], in_=w_t[s][:], func=ACT.Exp, scale=-1.0)
-
-        def drop(s):
-            engine = nc.gpsimd if s in D_G else nc.vector
-            if s == 0:
-                engine.tensor_scalar(out=dr[0][:], in0=tr[1][:], scalar1=-1.0, scalar2=1.0, op0=ALU.mult, op1=ALU.add)
-            elif s < S:
-                engine.tensor_tensor(out=dr[s][:], in0=tr[s][:], in1=tr[s + 1][:], op=ALU.subtract)
-            else:
-                engine.tensor_tensor(out=dr[s][:], in0=tr[s][:], in1=bg_b[:], op=ALU.mult)
+        def chain(s):
+            engine = nc.vector if s in T_V else nc.gpsimd
+            engine.tensor_tensor(out=tr[s + 1][:], in0=tr[s][:], in1=w_t[s][:], op=ALU.mult)
 
         c_t = [psum.tile([P, 4, P], F32, name="c%d" % c, tag="c%d" % c, bufs=1) for c in range(RT)]
         p_t = {}
@@ -194,21 +198,53 @@ def tile_spectralextinctionemissioncompositing_d1p_kernel(
         def emit_e(s):
             return [mm("xe", 4, s, c, we_w, we_s) for c in range(RT)]
 
-        def product(s, c, e):
-            p_t[c] = work.tile([P, F], F32, name="p%d" % c, tag="p%d" % c, bufs=3)
-            nc.vector.tensor_tensor(out=p_t[c][:], in0=dr[s][:, c, :], in1=e[c][:], op=ALU.mult)
+        turned = {0: 0, 1: 0}
+        n_turns = 2 * S - 1
 
-        def turn_add(s, c):
-            src = dr[s][:, c, :] if s == S else p_t[c][:]
+        def turn_add(c, src):
             for t in range(4):
                 nc.tensor.matmul(
                     out=c_t[c][:, t, :],
-                    lhsT=src[:, t:F:4],
+                    lhsT=src[:, 128 * t : 128 * (t + 1)],
                     rhs=ident[:],
                     is_transpose=True,
-                    start=(s == 0 and t == 0),
-                    stop=(s == S and t == 3),
+                    start=(turned[c] == 0 and t == 0),
+                    stop=(turned[c] == n_turns - 1 and t == 3),
                 )
+            turned[c] += 1
+
+        def product(s, c, e, scalar, op, after):
+            p = work.tile([P, F], F32, name="p", tag="p", bufs=6)
+            x = tr[s][:, c, :]
+            if after:
+                nc.vector.scalar_tensor_tensor(out=p[:], in0=x, scalar=scalar, in1=e[c][:], op0=op, op1=ALU.mult)
+            else:
+                nc.vector.tensor_tensor(out=p[:], in0=x, in1=e[c][:], op=ALU.mult)
+            return p
+
+        def products(s, e):
+            ps = []
+            if s == 0:
+                ps = [(c, product(1, c, e, 1.0, ALU.subtract, True)) for c in range(RT)]
+            else:
+                ps = [(c, product(s, c, e, -1.0, ALU.mult, True)) for c in range(RT)]
+                if s < S - 1:
+                    ps += [(c, product(s + 1, c, e, 0.0, ALU.mult, False)) for c in range(RT)]
+            return ps
+
+        def background(e):
+            for c in range(RT):
+                nc.vector.tensor_tensor(
+                    out=d7[:, c, :].rearrange("p (t q) -> p t q", t=4),
+                    in0=e[c][:].rearrange("p (t q) -> p t q", t=4),
+                    in1=bg_b[:, c, :].rearrange("p (q t) -> p t q", t=4),
+                    op=ALU.subtract,
+                )
+
+        def last_product(c):
+            p = work.tile([P, F], F32, name="p", tag="p", bufs=6)
+            nc.vector.tensor_tensor(out=p[:], in0=tr[S][:, c, :], in1=d7[:, c, :], op=ALU.mult)
+            return p
 
         fin = {}
 
@@ -217,7 +253,7 @@ def tile_spectralextinctionemissioncompositing_d1p_kernel(
             nc.vector.tensor_tensor(
                 out=g[:].rearrange("p (r t) -> p r t", t=4),
                 in0=c_t[c][:].rearrange("p t r -> p r t"),
-                in1=band_b[:].unsqueeze(1).broadcast_to([P, P, 4]),
+                in1=nband[:].unsqueeze(1).broadcast_to([P, P, 4]),
                 op=ALU.mult,
             )
             fin[c] = g
@@ -277,9 +313,16 @@ def tile_spectralextinctionemissioncompositing_d1p_kernel(
             batch = range(s0, s0 + n)
             s0 += n
             s_order += [("E", s) for s in batch] + [("L", s) for s in batch] + [("X", s) for s in batch]
-        s_call = {"E": exp_both, "L": log1p, "X": exp_depth}
+        s_call = {"E": exp_both, "L": log1p, "X": exp_tau}
         done = {"E": 0, "L": 0, "X": 0}
-        count = {"x": 0, "d": 0, "c": 0, "p": 0}
+        count = {"x": 0, "d": 0, "p": 0, "w": 0, "g": 0}
+
+        chained = [1]
+
+        def chain_ahead():
+            while chained[0] < done["X"] and chained[0] not in T_V:
+                chain(chained[0])
+                chained[0] += 1
 
         def advance_scalar(limit):
             for k in range(limit):
@@ -288,15 +331,13 @@ def tile_spectralextinctionemissioncompositing_d1p_kernel(
                 kind, s = s_order[0]
                 if kind == "E" and s >= count["x"]:
                     return
-                if kind == "X" and s >= count["c"]:
+                if kind == "X" and s >= count["d"]:
                     return
                 s_order.remove(s_order[0])
                 s_call[kind](s)
                 done[kind] = s + 1
-                if kind == "X" and s in D_G:
-                    drop(s)
-                if kind == "X" and s == S - 1 and S in D_G:
-                    drop(S)
+                if kind == "X":
+                    chain_ahead()
 
         e_t = {}
         for s in range(LEAD):
@@ -305,42 +346,46 @@ def tile_spectralextinctionemissioncompositing_d1p_kernel(
             deq_v(s, 0)
             deq_v(s, 1)
             turn(s)
-        v_drops = [s for s in range(S + 1) if s not in D_G]
+        permute_weight(ws_w, ws_s, ws_raw_w, ws_raw_s)
         for op in V_ORDER:
-            if op == "D":
-                s = v_drops[0]
-                v_drops.remove(s)
-                while done["X"] <= min(s, S - 1):
+            if op == "T":
+                while done["X"] <= chained[0]:
                     advance_scalar(1)
-                drop(s)
+                chain(chained[0])
+                chained[0] += 1
+                chain_ahead()
                 continue
             s = count[op]
             if op == "x":
                 prep(s)
+            if op == "w":
+                permute_weight(we_w, we_s, we_raw_w, we_raw_s)
+                nc.vector.tensor_scalar(out=nband[:], in0=band_b[:], scalar1=-1.0, scalar2=None, op0=ALU.mult)
+                nc.vector.tensor_scalar(
+                    out=ndl[:], in0=dl_b[:].rearrange("p c s -> p (c s)"), scalar1=-1.0, scalar2=None, op0=ALU.mult
+                )
+            if op == "g":
+                background(emit_e(S - 1))
             if op == "d":
                 while done["L"] <= s:
                     advance_scalar(1)
                 for c in range(RT):
                     softplus(s, c)
-            if op == "c":
-                for c in range(RT):
-                    depth(s, c)
             if op == "p":
                 while done["X"] <= s:
                     advance_scalar(1)
                 if s == 0:
                     e_t[0] = emit_e(0)
                     e_t[1] = emit_e(1)
-                for c in range(RT):
-                    product(s, c, e_t[s])
+                ps = products(s, e_t[s])
                 if s + 2 < S:
                     e_t[s + 2] = emit_e(s + 2)
-                for c in range(RT):
-                    turn_add(s, c)
+                for c, p in ps:
+                    turn_add(c, p[:])
             count[op] = s + 1
             advance_scalar(PACE)
         for c in range(RT):
-            turn_add(S, c)
+            turn_add(c, last_product(c)[:])
         for step in (finish_quant, finish_mx, finish_out):
             for c in range(RT):
                 step(c)

@@ -18,13 +18,12 @@ P = 128
 RT = R // P
 FLOPS = 2 * R * S * D * F * 2 + 2 * R * F * O
 
-BATCHES = (8,)
-DQ_S = (2, 4, 6, 7, 0, 2, 1, 2)
+BATCHES = (6, 2)
+DQ_S = (2, 8, 2, 3, 1, 0, 2, 0)
 LEAD = 3
 DR_S = ()
-T_V = (1,)
-V_ORDER = "xxxxxxxxwddddddddgpTppppppp"
-PACE = 2
+T_V = ()
+V_ORDER = "xxxxxxxxwddddddgppeqpeqpqdpdqpqpqp"
 CLAMP = 40.0
 
 
@@ -176,7 +175,7 @@ def tile_spectralextinctionemissioncompositing_d1p_kernel(
             nc.scalar.activation(out=t, in_=t, func=ACT.Ln, bias=1.0)
 
         def softplus(s, c):
-            v = mm("xe", 4, s, c, ws_w, ws_s)
+            v = mm("v", 2, s, c, ws_w, ws_s)
             t = w_t[s][:, c, :]
             nc.vector.scalar_tensor_tensor(out=t, in0=t, scalar=CLAMP, in1=v[:], op0=ALU.min, op1=ALU.max)
 
@@ -195,8 +194,8 @@ def tile_spectralextinctionemissioncompositing_d1p_kernel(
         c_t = [psum.tile([P, 4, P], F32, name="c%d" % c, tag="c%d" % c, bufs=1) for c in range(RT)]
         p_t = {}
 
-        def emit_e(s):
-            return [mm("xe", 4, s, c, we_w, we_s) for c in range(RT)]
+        def emit_e(s, tag="xe", bufs=4):
+            return [mm(tag, bufs, s, c, we_w, we_s) for c in range(RT)]
 
         turned = {0: 0, 1: 0}
         n_turns = 2 * S - 1
@@ -214,7 +213,7 @@ def tile_spectralextinctionemissioncompositing_d1p_kernel(
             turned[c] += 1
 
         def product(s, c, e, scalar, op, after):
-            p = work.tile([P, F], F32, name="p", tag="p", bufs=6)
+            p = work.tile([P, F], F32, name="p", tag="p", bufs=8)
             x = tr[s][:, c, :]
             if after:
                 nc.vector.scalar_tensor_tensor(out=p[:], in0=x, scalar=scalar, in1=e[c][:], op0=op, op1=ALU.mult)
@@ -223,14 +222,12 @@ def tile_spectralextinctionemissioncompositing_d1p_kernel(
             return p
 
         def products(s, e):
-            ps = []
             if s == 0:
-                ps = [(c, product(1, c, e, 1.0, ALU.subtract, True)) for c in range(RT)]
-            else:
-                ps = [(c, product(s, c, e, -1.0, ALU.mult, True)) for c in range(RT)]
-                if s < S - 1:
-                    ps += [(c, product(s + 1, c, e, 0.0, ALU.mult, False)) for c in range(RT)]
-            return ps
+                return [(c, product(1, c, e, 1.0, ALU.subtract, True)) for c in range(RT)]
+            return [(c, product(s, c, e, -1.0, ALU.mult, True)) for c in range(RT)]
+
+        def products_after(s, e):
+            return [(c, product(s + 1, c, e, 0.0, ALU.mult, False)) for c in range(RT)]
 
         def background(e):
             for c in range(RT):
@@ -242,7 +239,7 @@ def tile_spectralextinctionemissioncompositing_d1p_kernel(
                 )
 
         def last_product(c):
-            p = work.tile([P, F], F32, name="p", tag="p", bufs=6)
+            p = work.tile([P, F], F32, name="p", tag="p", bufs=8)
             nc.vector.tensor_tensor(out=p[:], in0=tr[S][:, c, :], in1=d7[:, c, :], op=ALU.mult)
             return p
 
@@ -307,16 +304,11 @@ def tile_spectralextinctionemissioncompositing_d1p_kernel(
             for c in range(RT):
                 exp_v(s, c)
 
-        s_order = []
-        s0 = 0
-        for n in BATCHES:
-            batch = range(s0, s0 + n)
-            s0 += n
-            s_order += [("E", s) for s in batch] + [("L", s) for s in batch] + [("X", s) for s in batch]
-        s_call = {"E": exp_both, "L": log1p, "X": exp_tau}
         done = {"E": 0, "L": 0, "X": 0}
-        count = {"x": 0, "d": 0, "p": 0, "w": 0, "g": 0}
-
+        count = {"x": 0, "d": 0, "e": 0, "p": 0, "q": 1, "w": 0, "g": 0}
+        ends = []
+        for n in BATCHES:
+            ends.append(n + (ends[-1] if ends else 0))
         chained = [1]
 
         def chain_ahead():
@@ -324,20 +316,13 @@ def tile_spectralextinctionemissioncompositing_d1p_kernel(
                 chain(chained[0])
                 chained[0] += 1
 
-        def advance_scalar(limit):
-            for k in range(limit):
-                if not s_order:
-                    return
-                kind, s = s_order[0]
-                if kind == "E" and s >= count["x"]:
-                    return
-                if kind == "X" and s >= count["d"]:
-                    return
-                s_order.remove(s_order[0])
-                s_call[kind](s)
-                done[kind] = s + 1
-                if kind == "X":
-                    chain_ahead()
+        def next_e():
+            exp_both(done["E"])
+            done["E"] += 1
+            if done["E"] in ends:
+                while done["L"] < done["E"]:
+                    log1p(done["L"])
+                    done["L"] += 1
 
         e_t = {}
         for s in range(LEAD):
@@ -347,17 +332,28 @@ def tile_spectralextinctionemissioncompositing_d1p_kernel(
             deq_v(s, 1)
             turn(s)
         permute_weight(ws_w, ws_s, ws_raw_w, ws_raw_s)
+        waiting = []
+
+        def flush(keep_last):
+            while len(waiting) > keep_last:
+                c, p = waiting[0]
+                waiting.remove(waiting[0])
+                turn_add(c, p[:])
+
         for op in V_ORDER:
             if op == "T":
-                while done["X"] <= chained[0]:
-                    advance_scalar(1)
                 chain(chained[0])
                 chained[0] += 1
                 chain_ahead()
                 continue
+            if op == "e":
+                next_e()
+                continue
             s = count[op]
             if op == "x":
                 prep(s)
+                if s < ends[0]:
+                    next_e()
             if op == "w":
                 permute_weight(we_w, we_s, we_raw_w, we_raw_s)
                 nc.vector.tensor_scalar(out=nband[:], in0=band_b[:], scalar1=-1.0, scalar2=None, op0=ALU.mult)
@@ -365,25 +361,23 @@ def tile_spectralextinctionemissioncompositing_d1p_kernel(
                     out=ndl[:], in0=dl_b[:].rearrange("p c s -> p (c s)"), scalar1=-1.0, scalar2=None, op0=ALU.mult
                 )
             if op == "g":
-                background(emit_e(S - 1))
+                background(emit_e(S - 1, "v", 2))
             if op == "d":
-                while done["L"] <= s:
-                    advance_scalar(1)
                 for c in range(RT):
                     softplus(s, c)
-            if op == "p":
-                while done["X"] <= s:
-                    advance_scalar(1)
-                if s == 0:
+                if s + 1 == ends[0]:
                     e_t[0] = emit_e(0)
-                    e_t[1] = emit_e(1)
-                ps = products(s, e_t[s])
-                if s + 2 < S:
-                    e_t[s + 2] = emit_e(s + 2)
-                for c, p in ps:
-                    turn_add(c, p[:])
+                exp_tau(s)
+                done["X"] += 1
+                chain_ahead()
+            if op in "pq":
+                for c, p in products(s, e_t[s]) if op == "p" else products_after(s, e_t[s]):
+                    waiting.append((c, p))
+                if op == "p" and s + 1 < S:
+                    e_t[s + 1] = emit_e(s + 1)
             count[op] = s + 1
-            advance_scalar(PACE)
+            flush(RT if op in "pq" else 0)
+        flush(0)
         for c in range(RT):
             turn_add(c, last_product(c)[:])
         for step in (finish_quant, finish_mx, finish_out):

@@ -19,11 +19,11 @@ RT = R // P
 FLOPS = 2 * R * S * D * F * 2 + 2 * R * F * O
 
 BATCHES = (6, 2)
-DQ_S = (2, 8, 2, 3, 1, 0, 2, 0)
+DQ_S = (2, 8, 2, 4, 1, 0, 2, 1)
 LEAD = 3
 DR_S = ()
-T_V = ()
-V_ORDER = "xxxxxxxxwddddddgppeqpeqpqdpdqpqpqp"
+T_V = (1,)
+V_ORDER = "xxxxxxxxwddddddgpTpeqpqepqdpdqpqpqp"
 CLAMP = 40.0
 
 
@@ -37,6 +37,24 @@ def tile_spectralextinctionemissioncompositing_d1p_kernel(
         psum = ctx.enter_context(tc.psum_pool(name="psum", bufs=2))
         ctx.enter_context(tc.manual_schedule())
 
+        def scale_tile(nm, width):
+            t = keep.tile([P, width], U8, name=nm, align_bytes=64)
+            nc.vector.memset(t[:].bitcast(I32), 0)
+            return t
+
+        def load_words(nm, src, width):
+            t = keep.tile([P, width], U32, name=nm, align_bytes=64)
+            nc.sync.dma_start(out=t[:].bitcast(I32), in_=src[0].rearrange("p n t -> p (n t)").bitcast(I32))
+            return t
+
+        def load_scales(t, src, queue):
+            for q in range(4):
+                queue.dma_start(
+                    out=t[32 * q : 32 * q + 4, :].bitcast(I32), in_=src[0, 4 * q : 4 * q + 4, :].bitcast(I32)
+                )
+
+        ws_raw_s = scale_tile("ws_raw_s", F)
+        load_scales(ws_raw_s, ws_scales, nc.scalar)
         warm = keep.tile([P, 1], F32, name="warm")
         nc.vector.memset(warm[:], 0.0)
         nc.scalar.activation(out=warm[:], in_=warm[:], func=ACT.Exp)
@@ -54,25 +72,8 @@ def tile_spectralextinctionemissioncompositing_d1p_kernel(
         x_tiles = {}
         x_tiles[0] = load_x(0)
 
-        def scale_tile(nm, width):
-            t = keep.tile([P, width], U8, name=nm, align_bytes=64)
-            nc.vector.memset(t[:].bitcast(I32), 0)
-            return t
-
-        def load_words(nm, src, width):
-            t = keep.tile([P, width], U32, name=nm, align_bytes=64)
-            nc.sync.dma_start(out=t[:].bitcast(I32), in_=src[0].rearrange("p n t -> p (n t)").bitcast(I32))
-            return t
-
-        def load_scales(t, src):
-            for q in range(4):
-                nc.sync.dma_start(
-                    out=t[32 * q : 32 * q + 4, :].bitcast(I32), in_=src[0, 4 * q : 4 * q + 4, :].bitcast(I32)
-                )
-
-        ws_raw_s = scale_tile("ws_raw_s", F)
         ws_raw_w = load_words("ws_raw_w", ws_words, F)
-        load_scales(ws_raw_s, ws_scales)
+
         x_tiles[2] = load_x(2)
         dl_b = keep.tile([P, RT, S], BF16, name="dl_b")
         nc.sync.dma_start(out=dl_b[:], in_=dl.rearrange("(c p) s -> p c s", p=P))
@@ -80,14 +81,14 @@ def tile_spectralextinctionemissioncompositing_d1p_kernel(
         x_tiles[6] = load_x(6)
         we_raw_s = scale_tile("we_raw_s", F)
         we_raw_w = load_words("we_raw_w", we_words, F)
-        load_scales(we_raw_s, we_scales)
+        load_scales(we_raw_s, we_scales, nc.sync)
         bg_b = keep.tile([P, RT, F], BF16, name="bg_b")
         nc.sync.dma_start(out=bg_b[:], in_=bg.rearrange("(c p) f -> p c f", p=P))
         band_b = keep.tile([P, 4], BF16, name="band_b")
         nc.sync.dma_start(out=band_b[:], in_=band.rearrange("(p t) -> p t", t=4))
         wm_s = scale_tile("wm_s", O)
         wm_w = load_words("wm_w", wm_words, O)
-        load_scales(wm_s, wm_scales)
+        load_scales(wm_s, wm_scales, nc.sync)
 
         ws_w = keep.tile([P, F], U32, name="ws_w", align_bytes=64)
         ws_s = keep.tile([P, F], U8, name="ws_s", align_bytes=64)
@@ -175,7 +176,7 @@ def tile_spectralextinctionemissioncompositing_d1p_kernel(
             nc.scalar.activation(out=t, in_=t, func=ACT.Ln, bias=1.0)
 
         def softplus(s, c):
-            v = mm("v", 2, s, c, ws_w, ws_s)
+            v = mm("xe", 4, s, c, ws_w, ws_s) if s < BATCHES[0] else mm("v", 2, s, c, ws_w, ws_s)
             t = w_t[s][:, c, :]
             nc.vector.scalar_tensor_tensor(out=t, in0=t, scalar=CLAMP, in1=v[:], op0=ALU.min, op1=ALU.max)
 
@@ -280,7 +281,8 @@ def tile_spectralextinctionemissioncompositing_d1p_kernel(
                     nc.scalar.copy(out=ob[:], in_=o[:])
                 else:
                     nc.vector.tensor_copy(out=ob[:], in_=o[:])
-                nc.sync.dma_start(out=out[c * P : (c + 1) * P, cols], in_=ob[:])
+                queue = nc.scalar if n == 0 else nc.sync
+                queue.dma_start(out=out[c * P : (c + 1) * P, cols], in_=ob[:])
 
         def deq_s(s):
             if s < S:

from contextlib import ExitStack

import concourse.mybir as mybir
from concourse.masks import make_identity

F32 = mybir.dt.float32
BF16 = mybir.dt.bfloat16
I32 = mybir.dt.int32
U32 = mybir.dt.uint32
U8 = mybir.dt.uint8
F8 = mybir.dt.float8_e4m3fn
X4 = mybir.dt.float8_e4m3fn_x4
ALU = mybir.AluOpType
ACT = mybir.ActivationFunctionType

R, S, D, F, O = 256, 8, 512, 512, 1024
P = 128
RT = R // P
FLOPS = 2 * R * S * D * F * 2 + 2 * R * F * O

BATCHES = (6, 2)
DQ_S = (2, 8, 2, 4, 1, 0, 2, 1)
LEAD = 3
DR_S = ()
T_V = (1,)
V_ORDER = "xxxxxxxxwddddddgpTpeqpqepqdpdqpqpqp"
CLAMP = 40.0


def tile_spectralextinctionemissioncompositing_d1p_kernel(
    tc, x_bytes, x_scale, we_words, we_scales, ws_words, ws_scales, dl, bg, band, wm_words, wm_scales, out
):
    nc = tc.nc
    with ExitStack() as ctx:
        keep = ctx.enter_context(tc.tile_pool(name="keep", bufs=1))
        work = ctx.enter_context(tc.tile_pool(name="work", bufs=2))
        psum = ctx.enter_context(tc.psum_pool(name="psum", bufs=2))
        ctx.enter_context(tc.manual_schedule())

        def scale_tile(nm, width):
            t = keep.tile([P, width], U8, name=nm, align_bytes=64)
            nc.vector.memset(t[:].bitcast(I32), 0)
            return t

        def load_words(nm, src, width):
            t = keep.tile([P, width], U32, name=nm, align_bytes=64)
            nc.sync.dma_start(out=t[:].bitcast(I32), in_=src[0].rearrange("p n t -> p (n t)").bitcast(I32))
            return t

        def load_scales(t, src, queue):
            for q in range(4):
                queue.dma_start(
                    out=t[32 * q : 32 * q + 4, :].bitcast(I32), in_=src[0, 4 * q : 4 * q + 4, :].bitcast(I32)
                )

        ws_raw_s = scale_tile("ws_raw_s", F)
        load_scales(ws_raw_s, ws_scales, nc.scalar)
        warm = keep.tile([P, 1], F32, name="warm")
        nc.vector.memset(warm[:], 0.0)
        nc.scalar.activation(out=warm[:], in_=warm[:], func=ACT.Exp)

        xs = keep.tile([P, RT, S * 4], F32, name="xs")
        nc.sync.dma_start(out=xs[:], in_=x_scale.rearrange("(c p) s j -> p c (s j)", p=P))
        xv = x_bytes.rearrange("(c p) s k -> p c s k", p=P)
        x8 = []

        def load_x(s0):
            t = keep.tile([P, RT, 2, D], U8, name="x8_%d" % s0)
            nc.sync.dma_start(out=t[:], in_=xv[:, :, s0 : s0 + 2, :])
            return t

        x_tiles = {}
        x_tiles[0] = load_x(0)

        ws_raw_w = load_words("ws_raw_w", ws_words, F)

        x_tiles[2] = load_x(2)
        dl_b = keep.tile([P, RT, S], BF16, name="dl_b")
        nc.sync.dma_start(out=dl_b[:], in_=dl.rearrange("(c p) s -> p c s", p=P))
        x_tiles[4] = load_x(4)
        x_tiles[6] = load_x(6)
        we_raw_s = scale_tile("we_raw_s", F)
        we_raw_w = load_words("we_raw_w", we_words, F)
        load_scales(we_raw_s, we_scales, nc.sync)
        bg_b = keep.tile([P, RT, F], BF16, name="bg_b")
        nc.sync.dma_start(out=bg_b[:], in_=bg.rearrange("(c p) f -> p c f", p=P))
        band_b = keep.tile([P, 4], BF16, name="band_b")
        nc.sync.dma_start(out=band_b[:], in_=band.rearrange("(p t) -> p t", t=4))
        wm_s = scale_tile("wm_s", O)
        wm_w = load_words("wm_w", wm_words, O)
        load_scales(wm_s, wm_scales, nc.sync)

        ws_w = keep.tile([P, F], U32, name="ws_w", align_bytes=64)
        ws_s = keep.tile([P, F], U8, name="ws_s", align_bytes=64)
        we_w = keep.tile([P, F], U32, name="we_w", align_bytes=64)
        we_s = keep.tile([P, F], U8, name="we_s", align_bytes=64)

        def permute(dst, src):
            nc.vector.tensor_copy(
                out=dst.rearrange("p (t q) -> p t q", t=4), in_=src.rearrange("p (q t) -> p t q", t=4)
            )

        def permute_weight(w, s, raw_w, raw_s):
            permute(w[:].bitcast(I32), raw_w[:].bitcast(I32))
            permute(s[:], raw_s[:])

        nband = keep.tile([P, 4], F32, name="nband")
        ndl = keep.tile([P, RT * S], F32, name="ndl")

        ident = keep.tile([P, P], F32, name="ident")
        make_identity(nc, ident[:])

        w_t = [keep.tile([P, RT, F], F32, name="w%d" % s) for s in range(S)]
        cx = [keep.tile([P, RT * P], U32, name="cx%d" % s, align_bytes=64) for s in range(S)]
        sx = [keep.tile([P, RT * P], U8, name="sx%d" % s, align_bytes=64) for s in range(S)]
        xb = {}
        gr = {}

        def deq(s, blocks, engine):
            if s not in xb:
                xb[s] = work.tile([P, RT, D], BF16, name="xb", tag="xb", bufs=5)
            src = x_tiles[s // 2 * 2]
            for b in blocks:
                c, j = divmod(b, 4)
                o = xb[s][:, c, 128 * j : 128 * (j + 1)]
                i = src[:, c, s % 2, 128 * j : 128 * (j + 1)].bitcast(F8)
                sc = xs[:, c, 4 * s + j : 4 * s + j + 1]
                if engine is nc.scalar:
                    nc.scalar.activation(out=o, in_=i, func=ACT.Copy, scale=sc)
                else:
                    nc.vector.tensor_scalar(out=o, in0=i, scalar1=sc, scalar2=None, op0=ALU.mult)

        def turn_words(src, dst):
            words = src.bitcast(F32)
            for u in range(2):
                nc.tensor.transpose(dst[:, u, :], words[:, u : D // 2 : 2], ident[:])

        xt = {}

        def turn(s):
            xt[s] = psum.tile([P, RT, 2, P], F32, name="xt", tag="xe", bufs=4)
            for c in range(RT):
                turn_words(xb[s][:, c, :], xt[s][:, c])

        def drain(s, engine):
            gr[s] = work.tile([P, RT * P * 2], F32, name="gr", tag="gr", bufs=2, align_bytes=64)
            copy = nc.scalar.copy if engine is nc.scalar else nc.vector.tensor_copy
            copy(
                out=gr[s][:].rearrange("p (c r u) -> p c r u", c=RT, u=2),
                in_=xt[s][:].rearrange("p c u r -> p c r u"),
            )

        def quant(s):
            nc.vector.quantize_mx(out=cx[s][:].bitcast(X4), scales=sx[s][:], in_=gr[s][:].bitcast(BF16))

        def mm(tag, bufs, s, c, w, sc):
            t = psum.tile([P, F], F32, name=tag, tag=tag, bufs=bufs)
            cols = slice(c * P, (c + 1) * P)
            nc.tensor.matmul_mx(
                out=t[:],
                lhsT=cx[s][:, cols].bitcast(X4),
                lhsT_scale=sx[s][:, cols],
                rhs=w[:].bitcast(X4),
                rhs_scale=sc[:],
                start=True,
                stop=True,
            )
            return t

        def exp_v(s, c):
            v = mm("v", 2, s, c, ws_w, ws_s)
            nc.scalar.activation(out=w_t[s][:, c, :], in_=v[:], func=ACT.Exp)

        def log1p(s):
            t = w_t[s][:].rearrange("p c f -> p (c f)")
            nc.scalar.activation(out=t, in_=t, func=ACT.Ln, bias=1.0)

        def softplus(s, c):
            v = mm("xe", 4, s, c, ws_w, ws_s) if s < BATCHES[0] else mm("v", 2, s, c, ws_w, ws_s)
            t = w_t[s][:, c, :]
            nc.vector.scalar_tensor_tensor(out=t, in0=t, scalar=CLAMP, in1=v[:], op0=ALU.min, op1=ALU.max)

        tr = [None, w_t[0]] + [keep.tile([P, RT, F], F32, name="tr%d" % s) for s in range(2, S + 1)]
        d7 = keep.tile([P, RT, F], F32, name="d7")

        def exp_tau(s):
            for c in range(RT):
                t = w_t[s][:, c, :]
                nc.scalar.activation(out=t, in_=t, func=ACT.Exp, scale=ndl[:, c * S + s : c * S + s + 1])

        def chain(s):
            engine = nc.vector if s in T_V else nc.gpsimd
            engine.tensor_tensor(out=tr[s + 1][:], in0=tr[s][:], in1=w_t[s][:], op=ALU.mult)

        c_t = [psum.tile([P, 4, P], F32, name="c%d" % c, tag="c%d" % c, bufs=1) for c in range(RT)]
        p_t = {}

        def emit_e(s, tag="xe", bufs=4):
            return [mm(tag, bufs, s, c, we_w, we_s) for c in range(RT)]

        turned = {0: 0, 1: 0}
        n_turns = 2 * S - 1

        def turn_add(c, src):
            for t in range(4):
                nc.tensor.matmul(
                    out=c_t[c][:, t, :],
                    lhsT=src[:, 128 * t : 128 * (t + 1)],
                    rhs=ident[:],
                    is_transpose=True,
                    start=(turned[c] == 0 and t == 0),
                    stop=(turned[c] == n_turns - 1 and t == 3),
                )
            turned[c] += 1

        def product(s, c, e, scalar, op, after):
            p = work.tile([P, F], F32, name="p", tag="p", bufs=8)
            x = tr[s][:, c, :]
            if after:
                nc.vector.scalar_tensor_tensor(out=p[:], in0=x, scalar=scalar, in1=e[c][:], op0=op, op1=ALU.mult)
            else:
                nc.vector.tensor_tensor(out=p[:], in0=x, in1=e[c][:], op=ALU.mult)
            return p

        def products(s, e):
            if s == 0:
                return [(c, product(1, c, e, 1.0, ALU.subtract, True)) for c in range(RT)]
            return [(c, product(s, c, e, -1.0, ALU.mult, True)) for c in range(RT)]

        def products_after(s, e):
            return [(c, product(s + 1, c, e, 0.0, ALU.mult, False)) for c in range(RT)]

        def background(e):
            for c in range(RT):
                nc.vector.tensor_tensor(
                    out=d7[:, c, :].rearrange("p (t q) -> p t q", t=4),
                    in0=e[c][:].rearrange("p (t q) -> p t q", t=4),
                    in1=bg_b[:, c, :].rearrange("p (q t) -> p t q", t=4),
                    op=ALU.subtract,
                )

        def last_product(c):
            p = work.tile([P, F], F32, name="p", tag="p", bufs=8)
            nc.vector.tensor_tensor(out=p[:], in0=tr[S][:, c, :], in1=d7[:, c, :], op=ALU.mult)
            return p

        fin = {}

        def finish_quant(c):
            g = work.tile([P, F], BF16, name="cg", tag="cg", bufs=2, align_bytes=64)
            nc.vector.tensor_tensor(
                out=g[:].rearrange("p (r t) -> p r t", t=4),
                in0=c_t[c][:].rearrange("p t r -> p r t"),
                in1=nband[:].unsqueeze(1).broadcast_to([P, P, 4]),
                op=ALU.mult,
            )
            fin[c] = g

        def finish_mx(c):
            cc = work.tile([P, P], U32, name="cc", tag="cc", bufs=2, align_bytes=64)
            cs = work.tile([P, P], U8, name="cs", tag="cs", bufs=2, align_bytes=64)
            nc.vector.quantize_mx(out=cc[:].bitcast(X4), scales=cs[:], in_=fin[c][:])
            fin[c] = (cc, cs)

        def finish_out(c):
            cc, cs = fin[c]
            for n in range(2):
                cols = slice(n * 512, (n + 1) * 512)
                o = psum.tile([P, 512], F32, name="o", tag="xe", bufs=4)
                nc.tensor.matmul_mx(
                    out=o[:],
                    lhsT=cc[:].bitcast(X4),
                    lhsT_scale=cs[:],
                    rhs=wm_w[:, cols].bitcast(X4),
                    rhs_scale=wm_s[:, cols],
                    start=True,
                    stop=True,
                )
                ob = work.tile([P, 512], F32, name="ob%d" % n, tag="ob%d" % n, bufs=2)
                if n == 0:
                    nc.scalar.copy(out=ob[:], in_=o[:])
                else:
                    nc.vector.tensor_copy(out=ob[:], in_=o[:])
                queue = nc.scalar if n == 0 else nc.sync
                queue.dma_start(out=out[c * P : (c + 1) * P, cols], in_=ob[:])

        def deq_s(s):
            if s < S:
                deq(s, range(8 - DQ_S[s], 8), nc.scalar)

        def deq_v(s, part):
            if s < S:
                n = 8 - DQ_S[s]
                deq(s, range(0, n // 2) if part == 0 else range(n // 2, n), nc.vector)

        def prep(s):
            deq_s(s + LEAD)
            deq_v(s + 2, 0)
            drain(s, nc.scalar if s in DR_S else nc.vector)
            deq_v(s + 2, 1)
            quant(s)
            if s + 2 < S:
                turn(s + 2)

        def exp_both(s):
            for c in range(RT):
                exp_v(s, c)

        done = {"E": 0, "L": 0, "X": 0}
        count = {"x": 0, "d": 0, "e": 0, "p": 0, "q": 1, "w": 0, "g": 0}
        ends = []
        for n in BATCHES:
            ends.append(n + (ends[-1] if ends else 0))
        chained = [1]

        def chain_ahead():
            while chained[0] < done["X"] and chained[0] not in T_V:
                chain(chained[0])
                chained[0] += 1

        def next_e():
            exp_both(done["E"])
            done["E"] += 1
            if done["E"] in ends:
                while done["L"] < done["E"]:
                    log1p(done["L"])
                    done["L"] += 1

        e_t = {}
        for s in range(LEAD):
            deq_s(s)
        for s in range(2):
            deq_v(s, 0)
            deq_v(s, 1)
            turn(s)
        permute_weight(ws_w, ws_s, ws_raw_w, ws_raw_s)
        waiting = []

        def flush(keep_last):
            while len(waiting) > keep_last:
                c, p = waiting[0]
                waiting.remove(waiting[0])
                turn_add(c, p[:])

        for op in V_ORDER:
            if op == "T":
                chain(chained[0])
                chained[0] += 1
                chain_ahead()
                continue
            if op == "e":
                next_e()
                continue
            s = count[op]
            if op == "x":
                prep(s)
                if s < ends[0]:
                    next_e()
            if op == "w":
                permute_weight(we_w, we_s, we_raw_w, we_raw_s)
                nc.vector.tensor_scalar(out=nband[:], in0=band_b[:], scalar1=-1.0, scalar2=None, op0=ALU.mult)
                nc.vector.tensor_scalar(
                    out=ndl[:], in0=dl_b[:].rearrange("p c s -> p (c s)"), scalar1=-1.0, scalar2=None, op0=ALU.mult
                )
            if op == "g":
                background(emit_e(S - 1, "v", 2))
            if op == "d":
                for c in range(RT):
                    softplus(s, c)
                if s + 1 == ends[0]:
                    e_t[0] = emit_e(0)
                exp_tau(s)
                done["X"] += 1
                chain_ahead()
            if op in "pq":
                for c, p in products(s, e_t[s]) if op == "p" else products_after(s, e_t[s]):
                    waiting.append((c, p))
                if op == "p" and s + 1 < S:
                    e_t[s + 1] = emit_e(s + 1)
            count[op] = s + 1
            flush(RT if op in "pq" else 0)
        flush(0)
        for c in range(RT):
            turn_add(c, last_product(c)[:])
        for step in (finish_quant, finish_mx, finish_out):
            for c in range(RT):
                step(c)
